import numpy as np, ml_dtypes
CORES = [8,136,40,168]
N = 4
import mx_ref
NC, G = 512, 2
C = np.float32(0.047)
BF = ml_dtypes.bfloat16
def cut(t, i, w=512):
    return t[:, w * i:w * i + w]
def tile(rs):
    return np.stack(rs, axis=2).reshape(128, -1).astype(BF)
def fold(P):
    return [f(p, axis=0) * C for p in P for f in (np.max, np.min)]
def setup_inputs(rng):
    def f(*shape):
        return mx_ref.flush((rng.standard_normal(shape, dtype=np.float32) * np.exp2(rng.integers(-2, 3, shape[:-1] + (1,)))).astype(BF))
    return {"x": f(N, 128, 4 * NC), "w1": f(N, 128, G * 512), "w2": f(N, 128, 2 * 512)}
def setup_inputs_blocks(rng):
    d = setup_inputs(rng)
    for k in ("x", "w1", "w2"): d[k] = mx_ref.spread(d[k], rng, 4)
    return d
def setup_inputs_wide(rng):
    d = setup_inputs(rng)
    for k in ("x", "w1", "w2"): d[k] = mx_ref.flush((d[k].astype(np.float32) * np.exp2(rng.integers(-8, 9, (N, 1, 1))).astype(np.float32)).astype(BF))
    return d
def reference(x, w1, w2, own=None):
    X = [mx_ref.quantize(x[j]) for j in range(N)]
    h = np.stack([tile(fold([[mx_ref.matmul(mx_ref.quantize(cut(w1[r], i)), X[j]) for j in range(N)] for i in range(G)])) for r in range(N)])
    use = h if own is None else own["h"]
    H = [mx_ref.quantize(use[j]) for j in range(N)]
    y = np.zeros((N, 128, NC), np.float32)
    for r in range(N):
        y[r] = mx_ref.matmul(mx_ref.quantize(cut(w2[r], 0)), H[r]) + mx_ref.matmul(mx_ref.quantize(cut(w2[r], 1)), H[(r + 1) % N])
    return {"h": h, "y": y}

@@ -1,0 +1,197 @@
+import numpy as np
+from concourse.mybir import dt, AluOpType, ActivationFunctionType
+
+N = 4
+NC = 512
+CH = [(0, 256), (256, 512)]
+CSCALE = float(np.float32(0.047))
+NEV = 80
+
+SCRATCH = {
+    "xt": ("sbuf", [128, 4 * NC], "bfloat16"),
+    "w1t": ("sbuf", [128, 1024], "bfloat16"),
+    "w2t": ("sbuf", [128, 1024], "bfloat16"),
+    "xq": ("sbuf", [128, N * NC], "float8_e4m3fn_x4"),
+    "xs": ("sbuf", [128, N * NC], "uint8"),
+    "w1q": ("sbuf", [128, 256], "float8_e4m3fn_x4"),
+    "w1s": ("sbuf", [128, 256], "uint8"),
+    "w2q": ("sbuf", [128, 256], "float8_e4m3fn_x4"),
+    "w2s": ("sbuf", [128, 256], "uint8"),
+    "ht": ("sbuf", [128, 4 * NC], "bfloat16"),
+    "hq": ("sbuf", [128, 2 * NC], "float8_e4m3fn_x4"),
+    "hs": ("sbuf", [128, 2 * NC], "uint8"),
+    "sb": ("sbuf", [128, 2 * NC], "float32"),
+    "mx": ("sbuf", [128, 2 * NC], "float32"),
+    "mn": ("sbuf", [128, 2 * NC], "float32"),
+    "yt": ("sbuf", [128, NC], "float32"),
+    "ps": ("psum", [128, 8 * 512], "float32"),
+}
+SEMAPHORES = (["ax%d" % j for j in range(N)] + ["ah%d" % c for c in range(len(CH))] + ["ls"]
+              + ["e%d" % i for i in range(NEV)])
+
+
+def rank_program(g, core, T, topo):
+    R = T.rank_of(core)
+    if R is None:
+        return
+    sem = T.sem
+    cnt = [0]
+
+    def ev():
+        s = sem["e%d" % cnt[0]]
+        cnt[0] += 1
+        return s
+
+    V, S, PE, SY = g.vector, g.scalar, g.tensor, g.sync
+    Copy = ActivationFunctionType.Copy
+    u8 = dt.uint8
+
+    def slot(j, a=0, b=NC):
+        return slice(NC * j + a, NC * j + b)
+
+    def bank(b, n=512):
+        return T.ps[:, 512 * b:512 * b + n]
+
+    e_x, e_w1, e_w2 = ev(), ev(), ev()
+    SY.dma_start(T.xt[:], T.x[:]).then_inc(e_x, 16)
+    SY.dma_start(T.w1t[:], T.w1[:]).then_inc(e_w1, 16)
+    SY.dma_start(T.w2t[:], T.w2[:]).then_inc(e_w2, 16)
+    q_x, q_w1, q_w2 = ev(), ev(), ev()
+    V.wait_ge(e_x, 16)
+    V.quantize_mx(T.xq[:, slot(R)], T.xs[:, slot(R)], T.xt[:]).then_inc(q_x, 1)
+    V.wait_ge(e_w1, 16)
+    V.quantize_mx(T.w1q[:], T.w1s[:], T.w1t[:]).then_inc(q_w1, 1)
+    V.wait_ge(e_w2, 16)
+    V.quantize_mx(T.w2q[:], T.w2s[:], T.w2t[:]).then_inc(q_w2, 1)
+
+    left = [0]
+
+    def send(dst, out_c, in_c, out_s, in_s, rsem):
+        rid, pid = topo.addr(dst, core)
+        m = topo.mask(core, dst)
+        g.remote_dma(out_c.bitcast(u8), in_c.bitcast(u8), rsem, sem.ls, pid, rid, m)
+        g.remote_dma(out_s, in_s, rsem, sem.ls, pid, rid, m)
+        left[0] += 2 * bin(m).count("1")
+        return 2 * bin(m).count("1")
+
+    g.wait_ge(q_x, 1)
+    for k in range(1, N):
+        send(T.cores[(R + k) % N], T.xq[:, slot(R)], T.xq[:, slot(R)], T.xs[:, slot(R)], T.xs[:, slot(R)],
+             sem["ax%d" % R])
+
+    def arrives(src):
+        return 2 * bin(topo.mask(src, core)).count("1")
+
+    def w1(i):
+        return T.w1q[:, 128 * i:128 * i + 128], T.w1s[:, 128 * i:128 * i + 128]
+
+    def w2(i):
+        return T.w2q[:, 128 * i:128 * i + 128], T.w2s[:, 128 * i:128 * i + 128]
+
+    rel = [[] for _ in range(8)]
+
+    def claim(b):
+        for s, n in rel[b]:
+            PE.wait_ge(s, n)
+        rel[b] = []
+
+    PE.wait_ge(q_x, 1)
+    PE.wait_ge(q_w1, 1)
+    p_own, c_own = ev(), ev()
+    for i in range(2):
+        a, b = w1(i)
+        PE.matmul_mx(bank(i), a, b, T.xq[:, slot(R)], T.xs[:, slot(R)], True, True).then_inc(p_own, 1)
+    S.wait_ge(p_own, 2)
+    S.activation(T.sb[:], T.ps[:, 0:1024], Copy).then_inc(c_own, 1)
+    rel[0].append((c_own, 1))
+    rel[1].append((c_own, 1))
+
+    prev = (c_own, 1)
+    for k in (1, 2):
+        j = (R - k) % N
+        p, f = ev(), ev()
+        PE.wait_ge(sem["ax%d" % j], arrives(T.cores[j]))
+        for i in range(2):
+            a, b = w1(i)
+            PE.matmul_mx(bank(2 * k + i), a, b, T.xq[:, slot(j)], T.xs[:, slot(j)], True, True).then_inc(p, 1)
+        V.wait_ge(p, 2)
+        V.wait_ge(prev[0], prev[1])
+        two = T.ps[:, 1024 * k:1024 * k + 1024]
+        V.tensor_tensor(T.mx[:], T.sb[:] if k == 1 else T.mx[:], two, AluOpType.max).then_inc(f, 1)
+        V.tensor_tensor(T.mn[:], T.sb[:] if k == 1 else T.mn[:], two, AluOpType.min).then_inc(f, 1)
+        rel[2 * k].append((f, 2))
+        rel[2 * k + 1].append((f, 2))
+        prev = (f, 2)
+
+    j = (R - 3) % N
+    PE.wait_ge(sem["ax%d" % j], arrives(T.cores[j]))
+    pairs = [(6, 7), (0, 1), (2, 3), (4, 5)]
+    p3 = []
+    for c, (c0, c1) in enumerate(CH):
+        ps_ = []
+        for i in range(2):
+            bk = pairs[c][i]
+            claim(bk)
+            a, b = w1(i)
+            e = ev()
+            PE.matmul_mx(bank(bk, c1 - c0), a, b, T.xq[:, slot(j, c0, c1)], T.xs[:, slot(j, c0, c1)],
+                         True, True).then_inc(e, 1)
+            ps_.append(e)
+        p3.append(ps_)
+    V.wait_ge(prev[0], prev[1])
+    qh, s3 = [], []
+    for c, (c0, c1) in enumerate(CH):
+        sc = ev()
+        for i in range(2):
+            bk = pairs[c][i]
+            V.wait_ge(p3[c][i], 1)
+            for t, (buf, op) in enumerate(((T.mx, AluOpType.max), (T.mn, AluOpType.min))):
+                f = ev()
+                view = buf[:, NC * i + c0:NC * i + c1]
+                V.tensor_tensor(view, view, bank(bk, c1 - c0), op).then_inc(f, 1)
+                rel[bk].append((f, 1))
+                S.wait_ge(f, 1)
+                S.activation(T.ht[:, 4 * c0 + 2 * i + t:4 * c1:4], view, Copy, scale=CSCALE).then_inc(sc, 1)
+        q = ev()
+        V.wait_ge(sc, 4)
+        V.quantize_mx(T.hq[:, c0:c1], T.hs[:, c0:c1], T.ht[:, 4 * c0:4 * c1]).then_inc(q, 1)
+        qh.append(q)
+        s3.append(sc)
+
+    dn = T.cores[(R - 1) % N]
+    up = T.cores[(R + 1) % N]
+    done = []
+    for c, (c0, c1) in enumerate(CH):
+        g.wait_ge(qh[c], 1)
+        send(dn, T.hq[:, NC + c0:NC + c1], T.hq[:, c0:c1], T.hs[:, NC + c0:NC + c1], T.hs[:, c0:c1], sem["ah%d" % c])
+        d = ev()
+        SY.wait_ge(s3[c], 4)
+        SY.dma_start(T.h[:, 4 * c0:4 * c1], T.ht[:, 4 * c0:4 * c1]).then_inc(d, 16)
+        done.append(d)
+
+    ybank = [6, 7, 0, 1]
+    PE.wait_ge(q_w2, 1)
+    for c, (c0, c1) in enumerate(CH):
+        claim(ybank[c])
+        PE.wait_ge(qh[c], 1)
+        a, b = w2(0)
+        PE.matmul_mx(bank(ybank[c], c1 - c0), a, b, T.hq[:, c0:c1], T.hs[:, c0:c1], True, False)
+    for c, (c0, c1) in enumerate(CH):
+        py, ey, d = ev(), ev(), ev()
+        PE.wait_ge(sem["ah%d" % c], arrives(up))
+        a, b = w2(1)
+        PE.matmul_mx(bank(ybank[c], c1 - c0), a, b, T.hq[:, NC + c0:NC + c1], T.hs[:, NC + c0:NC + c1],
+                     False, True).then_inc(py, 1)
+        if c % 2 == 0:
+            S.wait_ge(py, 1)
+            S.activation(T.yt[:, c0:c1], bank(ybank[c], c1 - c0), Copy).then_inc(ey, 1)
+        else:
+            V.wait_ge(py, 1)
+            V.tensor_copy(T.yt[:, c0:c1], bank(ybank[c], c1 - c0)).then_inc(ey, 1)
+        SY.wait_ge(ey, 1)
+        SY.dma_start(T.y[:, c0:c1], T.yt[:, c0:c1]).then_inc(d, 16)
+        done.append(d)
+
+    g.wait_ge(sem.ls, left[0])
+    for d in done:
+        g.wait_ge(d, 16)

@@ -4,6 +4,7 @@ from concourse.mybir import dt, AluOpType, ActivationFunctionType
 N = 4
 NC = 512
 CH = [(0, 256), (256, 512)]
+Q0 = 128
 CSCALE = float(np.float32(0.047))
 NEV = 80
 
@@ -26,7 +27,8 @@ SCRATCH = {
     "yt": ("sbuf", [128, NC], "float32"),
     "ps": ("psum", [128, 8 * 512], "float32"),
 }
-SEMAPHORES = (["ax%d" % j for j in range(N)] + ["ah%d" % c for c in range(len(CH))] + ["ls"]
+SEMAPHORES = (["ax%d" % j for j in range(N)] + ["ay%d" % j for j in range(N)]
+              + ["ah%d" % c for c in range(len(CH))] + ["lh%d" % c for c in range(len(CH))] + ["ls"]
               + ["e%d" % i for i in range(NEV)])
 
 
@@ -52,13 +54,16 @@ def rank_program(g, core, T, topo):
     def bank(b, n=512):
         return T.ps[:, 512 * b:512 * b + n]
 
-    e_x, e_w1, e_w2 = ev(), ev(), ev()
-    SY.dma_start(T.xt[:], T.x[:]).then_inc(e_x, 16)
+    e_x0, e_x1, e_w1, e_w2 = ev(), ev(), ev(), ev()
+    SY.dma_start(T.xt[:, 0:4 * Q0], T.x[:, 0:4 * Q0]).then_inc(e_x0, 16)
+    SY.dma_start(T.xt[:, 4 * Q0:4 * NC], T.x[:, 4 * Q0:4 * NC]).then_inc(e_x1, 16)
     SY.dma_start(T.w1t[:], T.w1[:]).then_inc(e_w1, 16)
     SY.dma_start(T.w2t[:], T.w2[:]).then_inc(e_w2, 16)
-    q_x, q_w1, q_w2 = ev(), ev(), ev()
-    V.wait_ge(e_x, 16)
-    V.quantize_mx(T.xq[:, slot(R)], T.xs[:, slot(R)], T.xt[:]).then_inc(q_x, 1)
+    q_x0, q_x, q_w1, q_w2 = ev(), ev(), ev(), ev()
+    V.wait_ge(e_x0, 16)
+    V.quantize_mx(T.xq[:, slot(R, 0, Q0)], T.xs[:, slot(R, 0, Q0)], T.xt[:, 0:4 * Q0]).then_inc(q_x0, 1)
+    V.wait_ge(e_x1, 16)
+    V.quantize_mx(T.xq[:, slot(R, Q0, NC)], T.xs[:, slot(R, Q0, NC)], T.xt[:, 4 * Q0:4 * NC]).then_inc(q_x, 1)
     V.wait_ge(e_w1, 16)
     V.quantize_mx(T.w1q[:], T.w1s[:], T.w1t[:]).then_inc(q_w1, 1)
     V.wait_ge(e_w2, 16)
@@ -66,21 +71,37 @@ def rank_program(g, core, T, topo):
 
     left = [0]
 
-    def send(dst, out_c, in_c, out_s, in_s, rsem):
+    def put(dst, out, in_, rsem, lsem=None):
         rid, pid = topo.addr(dst, core)
         m = topo.mask(core, dst)
-        g.remote_dma(out_c.bitcast(u8), in_c.bitcast(u8), rsem, sem.ls, pid, rid, m)
-        g.remote_dma(out_s, in_s, rsem, sem.ls, pid, rid, m)
-        left[0] += 2 * bin(m).count("1")
-        return 2 * bin(m).count("1")
+        g.remote_dma(out, in_, rsem, sem.ls if lsem is None else lsem, pid, rid, m)
+        if lsem is None:
+            left[0] += bin(m).count("1")
 
+    def xcodes(dst, a, b, rsem):
+        put(dst, T.xq[:, slot(R, a, b)].bitcast(u8), T.xq[:, slot(R, a, b)].bitcast(u8), rsem)
+
+    def xplane(dst, a, b, rsem):
+        put(dst, T.xs[:, slot(R, a, b)], T.xs[:, slot(R, a, b)], rsem)
+
+    ax, ay = sem["ax%d" % R], sem["ay%d" % R]
+    d1, d2, d3 = (T.cores[(R + k) % N] for k in (1, 2, 3))
+    HALF = CH[0][1]
+    g.wait_ge(q_x0, 1)
+    xplane(d1, 0, Q0, ax)
     g.wait_ge(q_x, 1)
-    for k in range(1, N):
-        send(T.cores[(R + k) % N], T.xq[:, slot(R)], T.xq[:, slot(R)], T.xs[:, slot(R)], T.xs[:, slot(R)],
-             sem["ax%d" % R])
+    xcodes(d1, 0, NC, ax)
+    xplane(d1, Q0, NC, ax)
+    xcodes(d2, 0, NC, ax)
+    xplane(d2, 0, NC, ax)
+    xplane(d3, 0, NC, ax)
+    xcodes(d3, 0, HALF, ax)
+    xcodes(d3, HALF, NC, ay)
 
-    def arrives(src):
-        return 2 * bin(topo.mask(src, core)).count("1")
+    def eng(src):
+        return bin(topo.mask(src, core)).count("1")
+
+    WRITES = {1: 3, 2: 2, 3: 2}
 
     def w1(i):
         return T.w1q[:, 128 * i:128 * i + 128], T.w1s[:, 128 * i:128 * i + 128]
@@ -95,6 +116,7 @@ def rank_program(g, core, T, topo):
             PE.wait_ge(s, n)
         rel[b] = []
 
+    PE.wait_ge(q_x0, 1)
     PE.wait_ge(q_x, 1)
     PE.wait_ge(q_w1, 1)
     p_own, c_own = ev(), ev()
@@ -110,7 +132,7 @@ def rank_program(g, core, T, topo):
     for k in (1, 2):
         j = (R - k) % N
         p, f = ev(), ev()
-        PE.wait_ge(sem["ax%d" % j], arrives(T.cores[j]))
+        PE.wait_ge(sem["ax%d" % j], WRITES[k] * eng(T.cores[j]))
         for i in range(2):
             a, b = w1(i)
             PE.matmul_mx(bank(2 * k + i), a, b, T.xq[:, slot(j)], T.xs[:, slot(j)], True, True).then_inc(p, 1)
@@ -124,11 +146,13 @@ def rank_program(g, core, T, topo):
         prev = (f, 2)
 
     j = (R - 3) % N
-    PE.wait_ge(sem["ax%d" % j], arrives(T.cores[j]))
+    PE.wait_ge(sem["ax%d" % j], WRITES[3] * eng(T.cores[j]))
     pairs = [(6, 7), (0, 1), (2, 3), (4, 5)]
     p3 = []
     for c, (c0, c1) in enumerate(CH):
         ps_ = []
+        if c == 1:
+            PE.wait_ge(sem["ay%d" % j], eng(T.cores[j]))
         for i in range(2):
             bk = pairs[c][i]
             claim(bk)
@@ -163,9 +187,12 @@ def rank_program(g, core, T, topo):
     done = []
     for c, (c0, c1) in enumerate(CH):
         g.wait_ge(qh[c], 1)
-        send(dn, T.hq[:, NC + c0:NC + c1], T.hq[:, c0:c1], T.hs[:, NC + c0:NC + c1], T.hs[:, c0:c1], sem["ah%d" % c])
+        lh = sem["lh%d" % c]
+        put(dn, T.hq[:, NC + c0:NC + c1].bitcast(u8), T.hq[:, c0:c1].bitcast(u8), sem["ah%d" % c], lh)
+        put(dn, T.hs[:, NC + c0:NC + c1], T.hs[:, c0:c1], sem["ah%d" % c], lh)
         d = ev()
         SY.wait_ge(s3[c], 4)
+        SY.wait_ge(lh, 2 * bin(topo.mask(core, dn)).count("1"))
         SY.dma_start(T.h[:, 4 * c0:4 * c1], T.ht[:, 4 * c0:4 * c1]).then_inc(d, 16)
         done.append(d)
 
@@ -178,7 +205,7 @@ def rank_program(g, core, T, topo):
         PE.matmul_mx(bank(ybank[c], c1 - c0), a, b, T.hq[:, c0:c1], T.hs[:, c0:c1], True, False)
     for c, (c0, c1) in enumerate(CH):
         py, ey, d = ev(), ev(), ev()
-        PE.wait_ge(sem["ah%d" % c], arrives(up))
+        PE.wait_ge(sem["ah%d" % c], 2 * eng(up))
         a, b = w2(1)
         PE.matmul_mx(bank(ybank[c], c1 - c0), a, b, T.hq[:, NC + c0:NC + c1], T.hs[:, NC + c0:NC + c1],
                      False, True).then_inc(py, 1)
@@ -188,8 +215,8 @@ def rank_program(g, core, T, topo):
         else:
             V.wait_ge(py, 1)
             V.tensor_copy(T.yt[:, c0:c1], bank(ybank[c], c1 - c0)).then_inc(ey, 1)
-        SY.wait_ge(ey, 1)
-        SY.dma_start(T.y[:, c0:c1], T.yt[:, c0:c1]).then_inc(d, 16)
+        S.wait_ge(ey, 1)
+        S.dma_start(T.y[:, c0:c1], T.yt[:, c0:c1]).then_inc(d, 16)
         done.append(d)
 
     g.wait_ge(sem.ls, left[0])

@@ -2,9 +2,9 @@ import numpy as np
 from concourse.mybir import dt, AluOpType, ActivationFunctionType
 
 N = 4
+NCORES = 256
 NC = 512
 CH = [(0, 256), (256, 512)]
-Q0 = 128
 CSCALE = float(np.float32(0.047))
 NEV = 80
 
@@ -28,15 +28,57 @@ SCRATCH = {
     "ps": ("psum", [128, 8 * 512], "float32"),
 }
 SEMAPHORES = (["ax%d" % j for j in range(N)] + ["ay%d" % j for j in range(N)]
-              + ["ah%d" % c for c in range(len(CH))] + ["lh%d" % c for c in range(len(CH))] + ["ls"]
+              + ["ah%d" % c for c in range(len(CH))] + ["lh", "ls"]
               + ["e%d" % i for i in range(NEV)])
 
 
+def ones(m):
+    return bin(m).count("1")
+
+
+def relay_of(topo, rc):
+    for c in range(NCORES):
+        if topo.host(c) == topo.host(rc) and topo.chip(c) == topo.chip(rc) and topo.die(c) != topo.die(rc):
+            return c
+
+
+def hand_mask(topo, rc, relay, far):
+    return topo.mask(rc, relay) & ~topo.mask(rc, far)
+
+
 def rank_program(g, core, T, topo):
+    sem = T.sem
+    u8 = dt.uint8
+    left = [0]
+
+    def slot(j, a=0, b=NC):
+        return slice(NC * j + a, NC * j + b)
+
+    def put(dst, out, in_, rsem, lsem=None, m=None):
+        rid, pid = topo.addr(dst, core)
+        if m is None:
+            m = topo.mask(core, dst)
+        g.remote_dma(out, in_, rsem, sem.ls if lsem is None else lsem, pid, rid, m)
+        if lsem is None:
+            left[0] += ones(m)
+
+    def xput(j, dst, c, m=None):
+        a, b = CH[c]
+        rsem = sem[("ax%d", "ay%d")[c] % j]
+        put(dst, T.xs[:, slot(j, a, b)], T.xs[:, slot(j, a, b)], rsem, None, m)
+        put(dst, T.xq[:, slot(j, a, b)].bitcast(u8), T.xq[:, slot(j, a, b)].bitcast(u8), rsem, None, m)
+
     R = T.rank_of(core)
     if R is None:
+        for r in range(N):
+            rc = T.cores[r]
+            if relay_of(topo, rc) == core:
+                g.wait_ge(sem["ay%d" % r], 2 * ones(hand_mask(topo, rc, core, T.cores[(r + 1) % N])))
+                xput(r, T.cores[(r + 2) % N], 1)
+                xput(r, T.cores[(r + 3) % N], 1)
+                g.wait_ge(sem.ls, left[0])
         return
-    sem = T.sem
+
     cnt = [0]
 
     def ev():
@@ -46,62 +88,41 @@ def rank_program(g, core, T, topo):
 
     V, S, PE, SY = g.vector, g.scalar, g.tensor, g.sync
     Copy = ActivationFunctionType.Copy
-    u8 = dt.uint8
-
-    def slot(j, a=0, b=NC):
-        return slice(NC * j + a, NC * j + b)
 
     def bank(b, n=512):
         return T.ps[:, 512 * b:512 * b + n]
 
-    e_x0, e_x1, e_w1, e_w2 = ev(), ev(), ev(), ev()
-    SY.dma_start(T.xt[:, 0:4 * Q0], T.x[:, 0:4 * Q0]).then_inc(e_x0, 16)
-    SY.dma_start(T.xt[:, 4 * Q0:4 * NC], T.x[:, 4 * Q0:4 * NC]).then_inc(e_x1, 16)
+    e_x = [ev(), ev()]
+    e_w1, e_w2 = ev(), ev()
+    for c, (c0, c1) in enumerate(CH):
+        SY.dma_start(T.xt[:, 4 * c0:4 * c1], T.x[:, 4 * c0:4 * c1]).then_inc(e_x[c], 16)
     SY.dma_start(T.w1t[:], T.w1[:]).then_inc(e_w1, 16)
     SY.dma_start(T.w2t[:], T.w2[:]).then_inc(e_w2, 16)
-    q_x0, q_x, q_w1, q_w2 = ev(), ev(), ev(), ev()
-    V.wait_ge(e_x0, 16)
-    V.quantize_mx(T.xq[:, slot(R, 0, Q0)], T.xs[:, slot(R, 0, Q0)], T.xt[:, 0:4 * Q0]).then_inc(q_x0, 1)
-    V.wait_ge(e_x1, 16)
-    V.quantize_mx(T.xq[:, slot(R, Q0, NC)], T.xs[:, slot(R, Q0, NC)], T.xt[:, 4 * Q0:4 * NC]).then_inc(q_x, 1)
+    q_x = [ev(), ev()]
+    q_w1, q_w2 = ev(), ev()
+    for c, (c0, c1) in enumerate(CH):
+        V.wait_ge(e_x[c], 16)
+        V.quantize_mx(T.xq[:, slot(R, c0, c1)], T.xs[:, slot(R, c0, c1)], T.xt[:, 4 * c0:4 * c1]).then_inc(q_x[c], 1)
     V.wait_ge(e_w1, 16)
     V.quantize_mx(T.w1q[:], T.w1s[:], T.w1t[:]).then_inc(q_w1, 1)
     V.wait_ge(e_w2, 16)
     V.quantize_mx(T.w2q[:], T.w2s[:], T.w2t[:]).then_inc(q_w2, 1)
 
-    left = [0]
-
-    def put(dst, out, in_, rsem, lsem=None):
-        rid, pid = topo.addr(dst, core)
-        m = topo.mask(core, dst)
-        g.remote_dma(out, in_, rsem, sem.ls if lsem is None else lsem, pid, rid, m)
-        if lsem is None:
-            left[0] += bin(m).count("1")
-
-    def xcodes(dst, a, b, rsem):
-        put(dst, T.xq[:, slot(R, a, b)].bitcast(u8), T.xq[:, slot(R, a, b)].bitcast(u8), rsem)
-
-    def xplane(dst, a, b, rsem):
-        put(dst, T.xs[:, slot(R, a, b)], T.xs[:, slot(R, a, b)], rsem)
-
-    ax, ay = sem["ax%d" % R], sem["ay%d" % R]
     d1, d2, d3 = (T.cores[(R + k) % N] for k in (1, 2, 3))
-    HALF = CH[0][1]
-    g.wait_ge(q_x0, 1)
-    xplane(d1, 0, Q0, ax)
-    g.wait_ge(q_x, 1)
-    xcodes(d1, 0, NC, ax)
-    xplane(d1, Q0, NC, ax)
-    xcodes(d2, 0, NC, ax)
-    xplane(d2, 0, NC, ax)
-    xplane(d3, 0, NC, ax)
-    xcodes(d3, 0, HALF, ax)
-    xcodes(d3, HALF, NC, ay)
+    relay = relay_of(topo, core)
+    g.wait_ge(q_x[0], 1)
+    xput(R, d1, 0)
+    g.wait_ge(q_x[1], 1)
+    xput(R, relay, 1, hand_mask(topo, core, relay, d1))
+    xput(R, d2, 0)
+    xput(R, d3, 0)
+    xput(R, d1, 1)
 
     def eng(src):
-        return bin(topo.mask(src, core)).count("1")
+        return ones(topo.mask(src, core))
 
-    WRITES = {1: 3, 2: 2, 3: 2}
+    def sender(j, c, k):
+        return relay_of(topo, T.cores[j]) if c == 1 and k > 1 else T.cores[j]
 
     def w1(i):
         return T.w1q[:, 128 * i:128 * i + 128], T.w1s[:, 128 * i:128 * i + 128]
@@ -116,8 +137,8 @@ def rank_program(g, core, T, topo):
             PE.wait_ge(s, n)
         rel[b] = []
 
-    PE.wait_ge(q_x0, 1)
-    PE.wait_ge(q_x, 1)
+    PE.wait_ge(q_x[0], 1)
+    PE.wait_ge(q_x[1], 1)
     PE.wait_ge(q_w1, 1)
     p_own, c_own = ev(), ev()
     for i in range(2):
@@ -127,55 +148,45 @@ def rank_program(g, core, T, topo):
     S.activation(T.sb[:], T.ps[:, 0:1024], Copy).then_inc(c_own, 1)
     rel[0].append((c_own, 1))
     rel[1].append((c_own, 1))
+    V.wait_ge(c_own, 1)
 
-    prev = (c_own, 1)
-    for k in (1, 2):
-        j = (R - k) % N
-        p, f = ev(), ev()
-        PE.wait_ge(sem["ax%d" % j], WRITES[k] * eng(T.cores[j]))
-        for i in range(2):
-            a, b = w1(i)
-            PE.matmul_mx(bank(2 * k + i), a, b, T.xq[:, slot(j)], T.xs[:, slot(j)], True, True).then_inc(p, 1)
-        V.wait_ge(p, 2)
-        V.wait_ge(prev[0], prev[1])
-        two = T.ps[:, 1024 * k:1024 * k + 1024]
-        V.tensor_tensor(T.mx[:], T.sb[:] if k == 1 else T.mx[:], two, AluOpType.max).then_inc(f, 1)
-        V.tensor_tensor(T.mn[:], T.sb[:] if k == 1 else T.mn[:], two, AluOpType.min).then_inc(f, 1)
-        rel[2 * k].append((f, 2))
-        rel[2 * k + 1].append((f, 2))
-        prev = (f, 2)
-
-    j = (R - 3) % N
-    PE.wait_ge(sem["ax%d" % j], WRITES[3] * eng(T.cores[j]))
-    pairs = [(6, 7), (0, 1), (2, 3), (4, 5)]
-    p3 = []
-    for c, (c0, c1) in enumerate(CH):
-        ps_ = []
-        if c == 1:
-            PE.wait_ge(sem["ay%d" % j], eng(T.cores[j]))
-        for i in range(2):
-            bk = pairs[c][i]
-            claim(bk)
-            a, b = w1(i)
-            e = ev()
-            PE.matmul_mx(bank(bk, c1 - c0), a, b, T.xq[:, slot(j, c0, c1)], T.xs[:, slot(j, c0, c1)],
-                         True, True).then_inc(e, 1)
-            ps_.append(e)
-        p3.append(ps_)
-    V.wait_ge(prev[0], prev[1])
+    pairs = [(2, 3), (4, 5), (6, 7)]
     qh, s3 = [], []
     for c, (c0, c1) in enumerate(CH):
+        n = c1 - c0
         sc = ev()
-        for i in range(2):
-            bk = pairs[c][i]
-            V.wait_ge(p3[c][i], 1)
-            for t, (buf, op) in enumerate(((T.mx, AluOpType.max), (T.mn, AluOpType.min))):
-                f = ev()
-                view = buf[:, NC * i + c0:NC * i + c1]
-                V.tensor_tensor(view, view, bank(bk, c1 - c0), op).then_inc(f, 1)
-                rel[bk].append((f, 1))
-                S.wait_ge(f, 1)
-                S.activation(T.ht[:, 4 * c0 + 2 * i + t:4 * c1:4], view, Copy, scale=CSCALE).then_inc(sc, 1)
+        prev = None
+        for k in (1, 2, 3):
+            j = (R - k) % N
+            pr = pairs[k - 1]
+            PE.wait_ge(sem[("ax%d", "ay%d")[c] % j], 2 * eng(sender(j, c, k)))
+            pe = []
+            for i in range(2):
+                claim(pr[i])
+                a, b = w1(i)
+                e = ev()
+                PE.matmul_mx(bank(pr[i], n), a, b, T.xq[:, slot(j, c0, c1)], T.xs[:, slot(j, c0, c1)],
+                             True, True).then_inc(e, 1)
+                pe.append(e)
+            if prev is not None:
+                V.wait_ge(prev, 4)
+            f = ev() if k < 3 else None
+            for i in range(2):
+                V.wait_ge(pe[i], 1)
+                for t, (buf, op) in enumerate(((T.mx, AluOpType.max), (T.mn, AluOpType.min))):
+                    view = buf[:, NC * i + c0:NC * i + c1]
+                    src = T.sb[:, NC * i + c0:NC * i + c1] if k == 1 else view
+                    if k < 3:
+                        V.tensor_tensor(view, src, bank(pr[i], n), op).then_inc(f, 1)
+                    else:
+                        fe = ev()
+                        V.tensor_tensor(view, src, bank(pr[i], n), op).then_inc(fe, 1)
+                        rel[pr[i]].append((fe, 1))
+                        S.wait_ge(fe, 1)
+                        S.activation(T.ht[:, 4 * c0 + 2 * i + t:4 * c1:4], view, Copy, scale=CSCALE).then_inc(sc, 1)
+                if k < 3:
+                    rel[pr[i]].append((f, 4))
+            prev = f
         q = ev()
         V.wait_ge(sc, 4)
         V.quantize_mx(T.hq[:, c0:c1], T.hs[:, c0:c1], T.ht[:, 4 * c0:4 * c1]).then_inc(q, 1)
@@ -185,25 +196,26 @@ def rank_program(g, core, T, topo):
     dn = T.cores[(R - 1) % N]
     up = T.cores[(R + 1) % N]
     done = []
+    last = len(CH) - 1
     for c, (c0, c1) in enumerate(CH):
         g.wait_ge(qh[c], 1)
-        lh = sem["lh%d" % c]
-        put(dn, T.hq[:, NC + c0:NC + c1].bitcast(u8), T.hq[:, c0:c1].bitcast(u8), sem["ah%d" % c], lh)
+        lh = sem.lh if c == last else None
         put(dn, T.hs[:, NC + c0:NC + c1], T.hs[:, c0:c1], sem["ah%d" % c], lh)
+        put(dn, T.hq[:, NC + c0:NC + c1].bitcast(u8), T.hq[:, c0:c1].bitcast(u8), sem["ah%d" % c], lh)
         d = ev()
         SY.wait_ge(s3[c], 4)
-        SY.wait_ge(lh, 2 * bin(topo.mask(core, dn)).count("1"))
+        if c == last:
+            SY.wait_ge(lh, 2 * ones(topo.mask(core, dn)))
         SY.dma_start(T.h[:, 4 * c0:4 * c1], T.ht[:, 4 * c0:4 * c1]).then_inc(d, 16)
         done.append(d)
 
-    ybank = [6, 7, 0, 1]
+    ybank = [0, 1]
     PE.wait_ge(q_w2, 1)
     for c, (c0, c1) in enumerate(CH):
         claim(ybank[c])
         PE.wait_ge(qh[c], 1)
         a, b = w2(0)
         PE.matmul_mx(bank(ybank[c], c1 - c0), a, b, T.hq[:, c0:c1], T.hs[:, c0:c1], True, False)
-    for c, (c0, c1) in enumerate(CH):
         py, ey, d = ev(), ev(), ev()
         PE.wait_ge(sem["ah%d" % c], 2 * eng(up))
         a, b = w2(1)

@@ -28,7 +28,7 @@ SCRATCH = {
     "ps": ("psum", [128, 8 * 512], "float32"),
 }
 SEMAPHORES = (["ax%d" % j for j in range(N)] + ["ay%d" % j for j in range(N)]
-              + ["ah%d" % c for c in range(len(CH))] + ["lh", "ls"]
+              + ["ah%d" % c for c in range(len(CH))] + ["rl%d" % i for i in range(4)] + ["lh", "ls"]
               + ["e%d" % i for i in range(NEV)])
 
 
@@ -62,20 +62,30 @@ def rank_program(g, core, T, topo):
         if lsem is None:
             left[0] += ones(m)
 
-    def xput(j, dst, c, m=None):
+    def xsem(j, c):
+        return sem[("ax%d", "ay%d")[c] % j]
+
+    def xplane(j, dst, c, rsem=None, m=None):
         a, b = CH[c]
-        rsem = sem[("ax%d", "ay%d")[c] % j]
-        put(dst, T.xs[:, slot(j, a, b)], T.xs[:, slot(j, a, b)], rsem, None, m)
-        put(dst, T.xq[:, slot(j, a, b)].bitcast(u8), T.xq[:, slot(j, a, b)].bitcast(u8), rsem, None, m)
+        put(dst, T.xs[:, slot(j, a, b)], T.xs[:, slot(j, a, b)], xsem(j, c) if rsem is None else rsem, None, m)
+
+    def xcodes(j, dst, c, rsem=None, m=None):
+        a, b = CH[c]
+        put(dst, T.xq[:, slot(j, a, b)].bitcast(u8), T.xq[:, slot(j, a, b)].bitcast(u8),
+            xsem(j, c) if rsem is None else rsem, None, m)
 
     R = T.rank_of(core)
     if R is None:
         for r in range(N):
             rc = T.cores[r]
             if relay_of(topo, rc) == core:
-                g.wait_ge(sem["ay%d" % r], 2 * ones(hand_mask(topo, rc, core, T.cores[(r + 1) % N])))
-                xput(r, T.cores[(r + 2) % N], 1)
-                xput(r, T.cores[(r + 3) % N], 1)
+                n = ones(hand_mask(topo, rc, core, T.cores[(r + 1) % N]))
+                far = T.cores[(r + 3) % N]
+                for c in range(2):
+                    g.wait_ge(sem["rl%d" % (2 * c)], n)
+                    xplane(r, far, c)
+                    g.wait_ge(sem["rl%d" % (2 * c + 1)], n)
+                    xcodes(r, far, c)
                 g.wait_ge(sem.ls, left[0])
         return
 
@@ -108,21 +118,29 @@ def rank_program(g, core, T, topo):
     V.wait_ge(e_w2, 16)
     V.quantize_mx(T.w2q[:], T.w2s[:], T.w2t[:]).then_inc(q_w2, 1)
 
-    d1, d2, d3 = (T.cores[(R + k) % N] for k in (1, 2, 3))
+    d1, d2 = (T.cores[(R + k) % N] for k in (1, 2))
     relay = relay_of(topo, core)
+    hm = hand_mask(topo, core, relay, d1)
     g.wait_ge(q_x[0], 1)
-    xput(R, d1, 0)
+    xplane(R, relay, 0, sem.rl0, hm)
+    xplane(R, d1, 0)
+    xcodes(R, d1, 0)
+    xcodes(R, relay, 0, sem.rl1, hm)
+    xplane(R, d2, 0)
+    xcodes(R, d2, 0)
     g.wait_ge(q_x[1], 1)
-    xput(R, relay, 1, hand_mask(topo, core, relay, d1))
-    xput(R, d2, 0)
-    xput(R, d3, 0)
-    xput(R, d1, 1)
+    xplane(R, relay, 1, sem.rl2, hm)
+    xcodes(R, relay, 1, sem.rl3, hm)
+    xplane(R, d1, 1)
+    xcodes(R, d1, 1)
+    xplane(R, d2, 1)
+    xcodes(R, d2, 1)
 
     def eng(src):
         return ones(topo.mask(src, core))
 
-    def sender(j, c, k):
-        return relay_of(topo, T.cores[j]) if c == 1 and k > 1 else T.cores[j]
+    def sender(j, k):
+        return relay_of(topo, T.cores[j]) if k == 3 else T.cores[j]
 
     def w1(i):
         return T.w1q[:, 128 * i:128 * i + 128], T.w1s[:, 128 * i:128 * i + 128]
@@ -151,47 +169,53 @@ def rank_program(g, core, T, topo):
     V.wait_ge(c_own, 1)
 
     pairs = [(2, 3), (4, 5), (6, 7)]
-    qh, s3 = [], []
-    for c, (c0, c1) in enumerate(CH):
+    sc = [ev(), ev()]
+    qh = [ev(), ev()]
+    prev = [None, None]
+    plan = [(0, 1), (0, 2), (0, 3), (1, 1), (None, 0), (1, 3), (1, 2), (None, 1)]
+    seen = [0, 0]
+    st = 0
+    for c, k in plan:
+        if c is None:
+            c0, c1 = CH[k]
+            V.wait_ge(sc[k], 4)
+            V.quantize_mx(T.hq[:, c0:c1], T.hs[:, c0:c1], T.ht[:, 4 * c0:4 * c1]).then_inc(qh[k], 1)
+            continue
+        c0, c1 = CH[c]
         n = c1 - c0
-        sc = ev()
-        prev = None
-        for k in (1, 2, 3):
-            j = (R - k) % N
-            pr = pairs[k - 1]
-            PE.wait_ge(sem[("ax%d", "ay%d")[c] % j], 2 * eng(sender(j, c, k)))
-            pe = []
-            for i in range(2):
-                claim(pr[i])
-                a, b = w1(i)
-                e = ev()
-                PE.matmul_mx(bank(pr[i], n), a, b, T.xq[:, slot(j, c0, c1)], T.xs[:, slot(j, c0, c1)],
-                             True, True).then_inc(e, 1)
-                pe.append(e)
-            if prev is not None:
-                V.wait_ge(prev, 4)
-            f = ev() if k < 3 else None
-            for i in range(2):
-                V.wait_ge(pe[i], 1)
-                for t, (buf, op) in enumerate(((T.mx, AluOpType.max), (T.mn, AluOpType.min))):
-                    view = buf[:, NC * i + c0:NC * i + c1]
-                    src = T.sb[:, NC * i + c0:NC * i + c1] if k == 1 else view
-                    if k < 3:
-                        V.tensor_tensor(view, src, bank(pr[i], n), op).then_inc(f, 1)
-                    else:
-                        fe = ev()
-                        V.tensor_tensor(view, src, bank(pr[i], n), op).then_inc(fe, 1)
-                        rel[pr[i]].append((fe, 1))
-                        S.wait_ge(fe, 1)
-                        S.activation(T.ht[:, 4 * c0 + 2 * i + t:4 * c1:4], view, Copy, scale=CSCALE).then_inc(sc, 1)
-                if k < 3:
-                    rel[pr[i]].append((f, 4))
-            prev = f
-        q = ev()
-        V.wait_ge(sc, 4)
-        V.quantize_mx(T.hq[:, c0:c1], T.hs[:, c0:c1], T.ht[:, 4 * c0:4 * c1]).then_inc(q, 1)
-        qh.append(q)
-        s3.append(sc)
+        seen[c] += 1
+        first, final = seen[c] == 1, seen[c] == N - 1
+        j = (R - k) % N
+        pr = pairs[st % 3]
+        st += 1
+        PE.wait_ge(xsem(j, c), 2 * eng(sender(j, k)))
+        pe = []
+        for i in range(2):
+            claim(pr[i])
+            a, b = w1(i)
+            e = ev()
+            PE.matmul_mx(bank(pr[i], n), a, b, T.xq[:, slot(j, c0, c1)], T.xs[:, slot(j, c0, c1)],
+                         True, True).then_inc(e, 1)
+            pe.append(e)
+        if prev[c] is not None:
+            V.wait_ge(prev[c], 4)
+        f = None if final else ev()
+        for i in range(2):
+            V.wait_ge(pe[i], 1)
+            for t, (buf, op) in enumerate(((T.mx, AluOpType.max), (T.mn, AluOpType.min))):
+                view = buf[:, NC * i + c0:NC * i + c1]
+                src = T.sb[:, NC * i + c0:NC * i + c1] if first else view
+                if not final:
+                    V.tensor_tensor(view, src, bank(pr[i], n), op).then_inc(f, 1)
+                else:
+                    fe = ev()
+                    V.tensor_tensor(view, src, bank(pr[i], n), op).then_inc(fe, 1)
+                    rel[pr[i]].append((fe, 1))
+                    S.wait_ge(fe, 1)
+                    S.activation(T.ht[:, 4 * c0 + 2 * i + t:4 * c1:4], view, Copy, scale=CSCALE).then_inc(sc[c], 1)
+            if not final:
+                rel[pr[i]].append((f, 4))
+        prev[c] = f
 
     dn = T.cores[(R - 1) % N]
     up = T.cores[(R + 1) % N]
@@ -203,7 +227,7 @@ def rank_program(g, core, T, topo):
         put(dn, T.hs[:, NC + c0:NC + c1], T.hs[:, c0:c1], sem["ah%d" % c], lh)
         put(dn, T.hq[:, NC + c0:NC + c1].bitcast(u8), T.hq[:, c0:c1].bitcast(u8), sem["ah%d" % c], lh)
         d = ev()
-        SY.wait_ge(s3[c], 4)
+        SY.wait_ge(sc[c], 4)
         if c == last:
             SY.wait_ge(lh, 2 * ones(topo.mask(core, dn)))
         SY.dma_start(T.h[:, 4 * c0:4 * c1], T.ht[:, 4 * c0:4 * c1]).then_inc(d, 16)

import numpy as np
from concourse.mybir import dt, AluOpType, ActivationFunctionType

N = 4
NCORES = 256
NC = 512
CH = [(0, 256), (256, 512)]
CSCALE = float(np.float32(0.047))
NEV = 80

SCRATCH = {
    "xt": ("sbuf", [128, 4 * NC], "bfloat16"),
    "w1t": ("sbuf", [128, 1024], "bfloat16"),
    "w2t": ("sbuf", [128, 1024], "bfloat16"),
    "xq": ("sbuf", [128, N * NC], "float8_e4m3fn_x4"),
    "xs": ("sbuf", [128, N * NC], "uint8"),
    "w1q": ("sbuf", [128, 256], "float8_e4m3fn_x4"),
    "w1s": ("sbuf", [128, 256], "uint8"),
    "w2q": ("sbuf", [128, 256], "float8_e4m3fn_x4"),
    "w2s": ("sbuf", [128, 256], "uint8"),
    "ht": ("sbuf", [128, 4 * NC], "bfloat16"),
    "hq": ("sbuf", [128, 2 * NC], "float8_e4m3fn_x4"),
    "hs": ("sbuf", [128, 2 * NC], "uint8"),
    "sb": ("sbuf", [128, 2 * NC], "float32"),
    "mx": ("sbuf", [128, 2 * NC], "float32"),
    "mn": ("sbuf", [128, 2 * NC], "float32"),
    "yt": ("sbuf", [128, NC], "float32"),
    "ps": ("psum", [128, 8 * 512], "float32"),
}
SEMAPHORES = (["ax%d" % j for j in range(N)] + ["ay%d" % j for j in range(N)]
              + ["ah%d" % c for c in range(len(CH))] + ["rl%d" % i for i in range(4)] + ["lh", "ls"]
              + ["e%d" % i for i in range(NEV)])


def ones(m):
    return bin(m).count("1")


def relay_of(topo, rc):
    for c in range(NCORES):
        if topo.host(c) == topo.host(rc) and topo.chip(c) == topo.chip(rc) and topo.die(c) != topo.die(rc):
            return c


def hand_mask(topo, rc, relay, far):
    return topo.mask(rc, relay) & ~topo.mask(rc, far)


def rank_program(g, core, T, topo):
    sem = T.sem
    u8 = dt.uint8
    left = [0]

    def slot(j, a=0, b=NC):
        return slice(NC * j + a, NC * j + b)

    def put(dst, out, in_, rsem, lsem=None, m=None):
        rid, pid = topo.addr(dst, core)
        if m is None:
            m = topo.mask(core, dst)
        g.remote_dma(out, in_, rsem, sem.ls if lsem is None else lsem, pid, rid, m)
        if lsem is None:
            left[0] += ones(m)

    def xsem(j, c):
        return sem[("ax%d", "ay%d")[c] % j]

    def xplane(j, dst, c, rsem=None, m=None):
        a, b = CH[c]
        put(dst, T.xs[:, slot(j, a, b)], T.xs[:, slot(j, a, b)], xsem(j, c) if rsem is None else rsem, None, m)

    def xcodes(j, dst, c, rsem=None, m=None):
        a, b = CH[c]
        put(dst, T.xq[:, slot(j, a, b)].bitcast(u8), T.xq[:, slot(j, a, b)].bitcast(u8),
            xsem(j, c) if rsem is None else rsem, None, m)

    R = T.rank_of(core)
    if R is None:
        for r in range(N):
            rc = T.cores[r]
            if relay_of(topo, rc) == core:
                n = ones(hand_mask(topo, rc, core, T.cores[(r + 1) % N]))
                far = T.cores[(r + 3) % N]
                for c in range(2):
                    g.wait_ge(sem["rl%d" % (2 * c)], n)
                    xplane(r, far, c)
                    g.wait_ge(sem["rl%d" % (2 * c + 1)], n)
                    xcodes(r, far, c)
                g.wait_ge(sem.ls, left[0])
        return

    cnt = [0]

    def ev():
        s = sem["e%d" % cnt[0]]
        cnt[0] += 1
        return s

    V, S, PE, SY = g.vector, g.scalar, g.tensor, g.sync
    Copy = ActivationFunctionType.Copy

    def bank(b, n=512):
        return T.ps[:, 512 * b:512 * b + n]

    e_x = [ev(), ev()]
    e_w1, e_w2 = ev(), ev()
    for c, (c0, c1) in enumerate(CH):
        SY.dma_start(T.xt[:, 4 * c0:4 * c1], T.x[:, 4 * c0:4 * c1]).then_inc(e_x[c], 16)
    SY.dma_start(T.w1t[:], T.w1[:]).then_inc(e_w1, 16)
    SY.dma_start(T.w2t[:], T.w2[:]).then_inc(e_w2, 16)
    q_x = [ev(), ev()]
    q_w1, q_w2 = ev(), ev()
    for c, (c0, c1) in enumerate(CH):
        V.wait_ge(e_x[c], 16)
        V.quantize_mx(T.xq[:, slot(R, c0, c1)], T.xs[:, slot(R, c0, c1)], T.xt[:, 4 * c0:4 * c1]).then_inc(q_x[c], 1)
    V.wait_ge(e_w1, 16)
    V.quantize_mx(T.w1q[:], T.w1s[:], T.w1t[:]).then_inc(q_w1, 1)
    V.wait_ge(e_w2, 16)
    V.quantize_mx(T.w2q[:], T.w2s[:], T.w2t[:]).then_inc(q_w2, 1)

    d1, d2 = (T.cores[(R + k) % N] for k in (1, 2))
    relay = relay_of(topo, core)
    hm = hand_mask(topo, core, relay, d1)
    g.wait_ge(q_x[0], 1)
    xplane(R, relay, 0, sem.rl0, hm)
    xplane(R, d1, 0)
    xcodes(R, d1, 0)
    xcodes(R, relay, 0, sem.rl1, hm)
    xplane(R, d2, 0)
    xcodes(R, d2, 0)
    g.wait_ge(q_x[1], 1)
    xplane(R, relay, 1, sem.rl2, hm)
    xcodes(R, relay, 1, sem.rl3, hm)
    xplane(R, d1, 1)
    xcodes(R, d1, 1)
    xplane(R, d2, 1)
    xcodes(R, d2, 1)

    def eng(src):
        return ones(topo.mask(src, core))

    def sender(j, k):
        return relay_of(topo, T.cores[j]) if k == 3 else T.cores[j]

    def w1(i):
        return T.w1q[:, 128 * i:128 * i + 128], T.w1s[:, 128 * i:128 * i + 128]

    def w2(i):
        return T.w2q[:, 128 * i:128 * i + 128], T.w2s[:, 128 * i:128 * i + 128]

    rel = [[] for _ in range(8)]

    def claim(b):
        for s, n in rel[b]:
            PE.wait_ge(s, n)
        rel[b] = []

    PE.wait_ge(q_x[0], 1)
    PE.wait_ge(q_x[1], 1)
    PE.wait_ge(q_w1, 1)
    p_own, c_own = ev(), ev()
    for i in range(2):
        a, b = w1(i)
        PE.matmul_mx(bank(i), a, b, T.xq[:, slot(R)], T.xs[:, slot(R)], True, True).then_inc(p_own, 1)
    S.wait_ge(p_own, 2)
    S.activation(T.sb[:], T.ps[:, 0:1024], Copy).then_inc(c_own, 1)
    rel[0].append((c_own, 1))
    rel[1].append((c_own, 1))
    V.wait_ge(c_own, 1)

    pairs = [(2, 3), (4, 5), (6, 7)]
    sc = [ev(), ev()]
    qh = [ev(), ev()]
    prev = [None, None]
    plan = [(0, 1), (0, 2), (0, 3), (1, 1), (None, 0), (1, 3), (1, 2), (None, 1)]
    seen = [0, 0]
    st = 0
    for c, k in plan:
        if c is None:
            c0, c1 = CH[k]
            V.wait_ge(sc[k], 4)
            V.quantize_mx(T.hq[:, c0:c1], T.hs[:, c0:c1], T.ht[:, 4 * c0:4 * c1]).then_inc(qh[k], 1)
            continue
        c0, c1 = CH[c]
        n = c1 - c0
        seen[c] += 1
        first, final = seen[c] == 1, seen[c] == N - 1
        j = (R - k) % N
        pr = pairs[st % 3]
        st += 1
        PE.wait_ge(xsem(j, c), 2 * eng(sender(j, k)))
        pe = []
        for i in range(2):
            claim(pr[i])
            a, b = w1(i)
            e = ev()
            PE.matmul_mx(bank(pr[i], n), a, b, T.xq[:, slot(j, c0, c1)], T.xs[:, slot(j, c0, c1)],
                         True, True).then_inc(e, 1)
            pe.append(e)
        if prev[c] is not None:
            V.wait_ge(prev[c], 4)
        f = None if final else ev()
        for i in range(2):
            V.wait_ge(pe[i], 1)
            for t, (buf, op) in enumerate(((T.mx, AluOpType.max), (T.mn, AluOpType.min))):
                view = buf[:, NC * i + c0:NC * i + c1]
                src = T.sb[:, NC * i + c0:NC * i + c1] if first else view
                if not final:
                    V.tensor_tensor(view, src, bank(pr[i], n), op).then_inc(f, 1)
                else:
                    fe = ev()
                    V.tensor_tensor(view, src, bank(pr[i], n), op).then_inc(fe, 1)
                    rel[pr[i]].append((fe, 1))
                    S.wait_ge(fe, 1)
                    S.activation(T.ht[:, 4 * c0 + 2 * i + t:4 * c1:4], view, Copy, scale=CSCALE).then_inc(sc[c], 1)
            if not final:
                rel[pr[i]].append((f, 4))
        prev[c] = f

    dn = T.cores[(R - 1) % N]
    up = T.cores[(R + 1) % N]
    done = []
    last = len(CH) - 1
    for c, (c0, c1) in enumerate(CH):
        g.wait_ge(qh[c], 1)
        lh = sem.lh if c == last else None
        put(dn, T.hs[:, NC + c0:NC + c1], T.hs[:, c0:c1], sem["ah%d" % c], lh)
        put(dn, T.hq[:, NC + c0:NC + c1].bitcast(u8), T.hq[:, c0:c1].bitcast(u8), sem["ah%d" % c], lh)
        d = ev()
        SY.wait_ge(sc[c], 4)
        if c == last:
            SY.wait_ge(lh, 2 * ones(topo.mask(core, dn)))
        SY.dma_start(T.h[:, 4 * c0:4 * c1], T.ht[:, 4 * c0:4 * c1]).then_inc(d, 16)
        done.append(d)

    ybank = [0, 1]
    PE.wait_ge(q_w2, 1)
    for c, (c0, c1) in enumerate(CH):
        claim(ybank[c])
        PE.wait_ge(qh[c], 1)
        a, b = w2(0)
        PE.matmul_mx(bank(ybank[c], c1 - c0), a, b, T.hq[:, c0:c1], T.hs[:, c0:c1], True, False)
        py, ey, d = ev(), ev(), ev()
        PE.wait_ge(sem["ah%d" % c], 2 * eng(up))
        a, b = w2(1)
        PE.matmul_mx(bank(ybank[c], c1 - c0), a, b, T.hq[:, NC + c0:NC + c1], T.hs[:, NC + c0:NC + c1],
                     False, True).then_inc(py, 1)
        if c % 2 == 0:
            S.wait_ge(py, 1)
            S.activation(T.yt[:, c0:c1], bank(ybank[c], c1 - c0), Copy).then_inc(ey, 1)
        else:
            V.wait_ge(py, 1)
            V.tensor_copy(T.yt[:, c0:c1], bank(ybank[c], c1 - c0)).then_inc(ey, 1)
        S.wait_ge(ey, 1)
        S.dma_start(T.y[:, c0:c1], T.yt[:, c0:c1]).then_inc(d, 16)
        done.append(d)

    g.wait_ge(sem.ls, left[0])
    for d in done:
        g.wait_ge(d, 16)
